import numpy as np
import ml_dtypes


def mxq(x, axis, fmt="e4m3"):
    dtype, down = {"e4m3": (ml_dtypes.float8_e4m3fn, 7), "e5m2": (ml_dtypes.float8_e5m2, 14)}[fmt]
    v = np.moveaxis(np.asarray(x, np.float32).astype(ml_dtypes.bfloat16).astype(np.float64), axis, -1)
    blocks = v.reshape(v.shape[:-1] + (-1, 32))
    amax = np.abs(blocks).max(-1, keepdims=True)
    byte = np.maximum(np.where(amax > 0, np.frexp(amax)[1] - 1 + 127, 0) - down, 1)
    scale = np.exp2(byte - 127.0)
    codes = (blocks / scale).astype(np.float32).astype(dtype).astype(np.float64)
    return np.moveaxis((codes * scale).reshape(v.shape), -1, axis)


WIDE = False


def mx_kscale(k):
    if not WIDE:
        return np.ones(k)
    levels = np.array([10, -10, 5, -5, 0])
    if k % 512:
        return np.exp2(np.random.permutation(np.resize(levels, k // 32))).repeat(32)
    a = np.empty((k // 512, 16))
    for p in range(k // 512):
        a[p, :8] = np.random.permutation(np.resize(levels, 8))
        for g in range(8):
            far = levels[np.abs(levels - a[p, g]) >= 10]
            a[p, g + 8] = far[np.random.randint(len(far))]
    return np.exp2(a.ravel()).repeat(32)


def f64(x):
    return np.asarray(x).astype(np.float64)


def striped(idx):
    return np.tile(idx.reshape(-1, 16).T, (8, 1)).astype(np.uint16)


def unstriped(offs):
    return offs[:16].T.reshape(-1).astype(np.int64)


E2M1 = np.array([0.0, 0.5, 1.0, 1.5, 2.0, 3.0, 4.0, 6.0, -0.0, -0.5, -1.0, -1.5, -2.0, -3.0, -4.0, -6.0])


def pack_fp4(w):
    k, n = w.shape
    w = f64(np.asarray(w, np.float32).astype(ml_dtypes.bfloat16)).reshape(k // 32, 32, n)
    amax = np.abs(w).max(1)
    mant, ex = np.frexp(amax / 6.0)
    byte = np.clip(np.where(amax > 0, np.where(mant > 0.5, ex, ex - 1) + 127, 1), 1, 254)
    scaled = (w * np.exp2(127.0 - byte)[:, None, :]).reshape(k, n).astype(np.float32)
    c = np.ascontiguousarray(scaled.reshape(k // 512, 128, 4, n).transpose(0, 1, 3, 2)).astype(ml_dtypes.float4_e2m1fn).view(np.uint8) & 0xF
    words = (c[..., 0::2] | (c[..., 1::2] << 4)).reshape(k // 512, 128, 2 * n)
    return np.ascontiguousarray(words), np.ascontiguousarray(byte.astype(np.uint8).reshape(k // 512, 16, n))


def unpack_fp4(words, scales):
    g, _, n = scales.shape
    words = np.ascontiguousarray(words).reshape(g, 128, n, 2)
    nib = np.empty((g, 128, n, 4), np.uint8)
    nib[..., 0::2] = words & 0xF
    nib[..., 1::2] = words >> 4
    vals = E2M1[nib] * np.repeat(np.exp2(scales.astype(np.float64) - 127.0), 8, axis=1)[..., None]
    return vals.transpose(0, 1, 3, 2).reshape(g * 512, n)


K, T, N = 512, 512, 128
P = 2 ** 7


def setup_inputs():
    n = np.random.standard_normal
    s = mx_kscale(K)[:, None]
    packed_xT = pack_fp4(n((K, T)) * s)
    return {
        "x_words": packed_xT[0],
        "x_scales": packed_xT[1],
        "w1": (n((K, N)) / np.sqrt(K) / s).astype(np.float32),
        "frac": np.tile(np.random.uniform(0.05, 0.95, T), (P, 1)).astype(np.float32),
        "left": striped(np.random.permutation(T)),
        "right": striped(np.random.permutation(T)),
    }


def reference(x_words, x_scales, w1, frac, left, right):
    xq = unpack_fp4(x_words, x_scales)
    y = mxq(f64(w1), 0, "e4m3").T @ xq
    l = y[:, unstriped(left)]
    return l + (y[:, unstriped(right)] - l) * f64(frac)[:1]

@@ -1,0 +1,88 @@
+from contextlib import ExitStack
+
+import concourse.mybir as mybir
+
+K, T, M = 512, 512, 128
+FLOPS = 2 * K * T * M
+
+F32 = mybir.dt.float32
+BF16 = mybir.dt.bfloat16
+I32 = mybir.dt.int32
+U32 = mybir.dt.uint32
+U16 = mybir.dt.uint16
+U8 = mybir.dt.uint8
+FP8X4 = mybir.dt.float8_e4m3fn_x4
+FP4X4 = mybir.dt.float4_e2m1fn_x4
+MULT = mybir.AluOpType.mult
+ADD = mybir.AluOpType.add
+IDENT = mybir.ActivationFunctionType.Identity
+COPY = mybir.ActivationFunctionType.Copy
+
+P = 128
+PACK = 4
+N_PASS = 128
+CHUNKS = (256, 256)
+
+
+def tile_picked_wlerp_none_l_kernel(tc, x_words, x_scales, w1, frac, left, right, out):
+    nc = tc.nc
+    with ExitStack() as ctx:
+        sb = ctx.enter_context(tc.tile_pool(name="sb", bufs=1))
+        psum = ctx.enter_context(tc.psum_pool(name="psum", bufs=1))
+
+        left_t = sb.tile([P, T // 16], U16, name="left_t")
+        right_t = sb.tile([P, T // 16], U16, name="right_t")
+        w_raw = sb.tile([P, PACK, M], F32, name="w_raw")
+        x_codes = sb.tile([P, 2 * T], U8, name="x_codes", align_bytes=64)
+        x_plane = sb.tile([P, T], U8, name="x_plane", align_bytes=64)
+        to_right = sb.tile([P, T], F32, name="to_right")
+        to_left = sb.tile([P, T], F32, name="to_left")
+
+        nc.sync.dma_start(out=w_raw[:], in_=w1.rearrange("(p j) m -> p j m", j=PACK))
+        nc.sync.dma_start(out=x_codes[:], in_=x_words[0])
+        nc.vector.memset(x_plane[:].bitcast(I32), 0)
+        for q in range(4):
+            (nc.scalar if q < 2 else nc.sync).dma_start(
+                out=x_plane[32 * q : 32 * q + 4, :].bitcast(I32), in_=x_scales[0, 4 * q : 4 * q + 4, :].bitcast(I32)
+            )
+        nc.sync.dma_start(out=to_right[:], in_=frac)
+        nc.sync.dma_start(right_t[:], right)
+        nc.sync.dma_start(left_t[:], left)
+
+        nc.scalar.activation(out=to_left[:], in_=to_right[:], func=COPY, scale=-1.0, bias=1.0)
+
+        w_bf = sb.tile([P, M * PACK], BF16, name="w_bf", align_bytes=64)
+        nc.vector.tensor_copy(
+            out=w_bf[:].rearrange("p (c i t) -> p c t i", i=4, t=PACK),
+            in_=w_raw[:].rearrange("p t (c i) -> p c t i", i=4),
+        )
+        w_codes = sb.tile([P, M], U32, name="w_codes", align_bytes=64)
+        w_plane = sb.tile([P, M], U8, name="w_plane", align_bytes=64)
+        nc.vector.quantize_mx(out=w_codes[:].bitcast(FP8X4), scales=w_plane[:], in_=w_bf[:])
+
+        y = sb.tile([P, T], F32, name="y")
+        for n0 in range(0, T, N_PASS):
+            bank = psum.tile([M, N_PASS], F32, name="bank%d" % n0)
+            nc.tensor.matmul_mx(
+                out=bank[:],
+                lhsT=w_codes[:].bitcast(FP8X4),
+                lhsT_scale=w_plane[:],
+                rhs=x_codes[:, 2 * n0 : 2 * (n0 + N_PASS)].bitcast(FP4X4),
+                rhs_scale=x_plane[:, n0 : n0 + N_PASS],
+                start=True,
+                stop=True,
+            )
+            nc.vector.tensor_copy(out=y[:, n0 : n0 + N_PASS], in_=bank[:])
+
+        v0 = 0
+        for i, n in enumerate(CHUNKS):
+            cols = slice(v0, v0 + n)
+            offs = slice(v0 // 16, (v0 + n) // 16)
+            a = sb.tile([P, n], F32, name="a%d" % i)
+            b = sb.tile([P, n], F32, name="b%d" % i)
+            o = sb.tile([P, n], F32, name="o%d" % i)
+            nc.vector.tensor_tensor(b[:], y[:].indirect(right_t[:, offs]), to_right[:, cols], MULT)
+            nc.vector.tensor_tensor(a[:], y[:].indirect(left_t[:, offs]), to_left[:, cols], MULT)
+            nc.vector.tensor_tensor(o[:], a[:], b[:], ADD)
+            nc.sync.dma_start(out=out[:, cols], in_=o[:])
+            v0 = v0 + n

@@ -15,13 +15,15 @@ FP8X4 = mybir.dt.float8_e4m3fn_x4
 FP4X4 = mybir.dt.float4_e2m1fn_x4
 MULT = mybir.AluOpType.mult
 ADD = mybir.AluOpType.add
-IDENT = mybir.ActivationFunctionType.Identity
 COPY = mybir.ActivationFunctionType.Copy
 
 P = 128
 PACK = 4
-N_PASS = 128
-CHUNKS = (256, 256)
+PASSES = (128, 128, 128, 128)
+SPARE = 0
+LEFT_CUTS = ()
+ADD_CUTS = ()
+W_CUTS = (128,)
 
 
 def tile_picked_wlerp_none_l_kernel(tc, x_words, x_scales, w1, frac, left, right, out):
@@ -37,10 +39,11 @@ def tile_picked_wlerp_none_l_kernel(tc, x_words, x_scales, w1, frac, left, right
         x_plane = sb.tile([P, T], U8, name="x_plane", align_bytes=64)
         to_right = sb.tile([P, T], F32, name="to_right")
         to_left = sb.tile([P, T], F32, name="to_left")
+        y = sb.tile([P, T + SPARE], F32, name="y")
 
+        nc.vector.memset(x_plane[:].bitcast(I32), 0)
         nc.sync.dma_start(out=w_raw[:], in_=w1.rearrange("(p j) m -> p j m", j=PACK))
         nc.sync.dma_start(out=x_codes[:], in_=x_words[0])
-        nc.vector.memset(x_plane[:].bitcast(I32), 0)
         for q in range(4):
             (nc.scalar if q < 2 else nc.sync).dma_start(
                 out=x_plane[32 * q : 32 * q + 4, :].bitcast(I32), in_=x_scales[0, 4 * q : 4 * q + 4, :].bitcast(I32)
@@ -52,37 +55,54 @@ def tile_picked_wlerp_none_l_kernel(tc, x_words, x_scales, w1, frac, left, right
         nc.scalar.activation(out=to_left[:], in_=to_right[:], func=COPY, scale=-1.0, bias=1.0)
 
         w_bf = sb.tile([P, M * PACK], BF16, name="w_bf", align_bytes=64)
-        nc.vector.tensor_copy(
-            out=w_bf[:].rearrange("p (c i t) -> p c t i", i=4, t=PACK),
-            in_=w_raw[:].rearrange("p t (c i) -> p c t i", i=4),
-        )
         w_codes = sb.tile([P, M], U32, name="w_codes", align_bytes=64)
         w_plane = sb.tile([P, M], U8, name="w_plane", align_bytes=64)
-        nc.vector.quantize_mx(out=w_codes[:].bitcast(FP8X4), scales=w_plane[:], in_=w_bf[:])
+        m0 = 0
+        for n in W_CUTS:
+            nc.vector.tensor_copy(
+                out=w_bf[:, PACK * m0 : PACK * (m0 + n)].rearrange("p (c i t) -> p c t i", i=4, t=PACK),
+                in_=w_raw[:, :, m0 : m0 + n].rearrange("p t (c i) -> p c t i", i=4),
+            )
+            m0 = m0 + n
+        m0 = 0
+        for n in W_CUTS:
+            nc.vector.quantize_mx(
+                out=w_codes[:, m0 : m0 + n].bitcast(FP8X4),
+                scales=w_plane[:, m0 : m0 + n],
+                in_=w_bf[:, PACK * m0 : PACK * (m0 + n)],
+            )
+            m0 = m0 + n
 
-        y = sb.tile([P, T], F32, name="y")
-        for n0 in range(0, T, N_PASS):
-            bank = psum.tile([M, N_PASS], F32, name="bank%d" % n0)
+        n0 = 0
+        for i, n in enumerate(PASSES):
+            bank = psum.tile([M, n], F32, name="bank%d" % i)
             nc.tensor.matmul_mx(
                 out=bank[:],
                 lhsT=w_codes[:].bitcast(FP8X4),
                 lhsT_scale=w_plane[:],
-                rhs=x_codes[:, 2 * n0 : 2 * (n0 + N_PASS)].bitcast(FP4X4),
-                rhs_scale=x_plane[:, n0 : n0 + N_PASS],
+                rhs=x_codes[:, 2 * n0 : 2 * (n0 + n)].bitcast(FP4X4),
+                rhs_scale=x_plane[:, n0 : n0 + n],
                 start=True,
                 stop=True,
             )
-            nc.vector.tensor_copy(out=y[:, n0 : n0 + N_PASS], in_=bank[:])
+            nc.vector.tensor_copy(out=y[:, n0 : n0 + n], in_=bank[:])
+            n0 = n0 + n
 
-        v0 = 0
-        for i, n in enumerate(CHUNKS):
-            cols = slice(v0, v0 + n)
-            offs = slice(v0 // 16, (v0 + n) // 16)
-            a = sb.tile([P, n], F32, name="a%d" % i)
-            b = sb.tile([P, n], F32, name="b%d" % i)
-            o = sb.tile([P, n], F32, name="o%d" % i)
-            nc.vector.tensor_tensor(b[:], y[:].indirect(right_t[:, offs]), to_right[:, cols], MULT)
-            nc.vector.tensor_tensor(a[:], y[:].indirect(left_t[:, offs]), to_left[:, cols], MULT)
-            nc.vector.tensor_tensor(o[:], a[:], b[:], ADD)
-            nc.sync.dma_start(out=out[:, cols], in_=o[:])
-            v0 = v0 + n
+        from_right = sb.tile([P, T], F32, name="from_right")
+        from_left = sb.tile([P, T], F32, name="from_left")
+        result = sb.tile([P, T], F32, name="result")
+
+        def gather(dst, offsets, weight, v0, v1):
+            nc.vector.tensor_tensor(dst[:, v0:v1], y[:].indirect(offsets[:, v0 // 16 : v1 // 16]), weight[:, v0:v1], MULT)
+
+        def finish(v0, v1):
+            nc.vector.tensor_tensor(result[:, v0:v1], from_left[:, v0:v1], from_right[:, v0:v1], ADD)
+            nc.sync.dma_start(out=out[:, v0:v1], in_=result[:, v0:v1])
+
+        gather(from_right, right_t, to_right, 0, 384)
+        gather(from_left, left_t, to_left, 0, 384)
+        gather(from_right, right_t, to_right, 384, 512)
+        finish(0, 192)
+        gather(from_left, left_t, to_left, 384, 512)
+        finish(192, 384)
+        finish(384, 512)

@@ -23,7 +23,7 @@ PASSES = (128, 128, 128, 128)
 SPARE = 0
 LEFT_CUTS = ()
 ADD_CUTS = ()
-W_CUTS = (128,)
+W_CUTS = (64, 64)
 
 
 def tile_picked_wlerp_none_l_kernel(tc, x_words, x_scales, w1, frac, left, right, out):

@@ -19,11 +19,9 @@ COPY = mybir.ActivationFunctionType.Copy
 
 P = 128
 PACK = 4
+HALF = 64
 PASSES = (128, 128, 128, 128)
-SPARE = 0
-LEFT_CUTS = ()
-ADD_CUTS = ()
-W_CUTS = (64, 64)
+S_BANKS = ()
 
 
 def tile_picked_wlerp_none_l_kernel(tc, x_words, x_scales, w1, frac, left, right, out):
@@ -34,44 +32,50 @@ def tile_picked_wlerp_none_l_kernel(tc, x_words, x_scales, w1, frac, left, right
 
         left_t = sb.tile([P, T // 16], U16, name="left_t")
         right_t = sb.tile([P, T // 16], U16, name="right_t")
-        w_raw = sb.tile([P, PACK, M], F32, name="w_raw")
         x_codes = sb.tile([P, 2 * T], U8, name="x_codes", align_bytes=64)
         x_plane = sb.tile([P, T], U8, name="x_plane", align_bytes=64)
         to_right = sb.tile([P, T], F32, name="to_right")
         to_left = sb.tile([P, T], F32, name="to_left")
-        y = sb.tile([P, T + SPARE], F32, name="y")
+        y = sb.tile([P, T], F32, name="y")
+        w_bf = sb.tile([P, M * PACK], BF16, name="w_bf", align_bytes=64)
+        w_codes = sb.tile([P, M], U32, name="w_codes", align_bytes=64)
+        w_plane = sb.tile([P, M], U8, name="w_plane", align_bytes=64)
+        from_right = sb.tile([P, T], F32, name="from_right")
+        from_left = sb.tile([P, T], F32, name="from_left")
+        result = sb.tile([P, T], F32, name="result")
 
+        w_rows = w1.rearrange("(p j) m -> p j m", j=PACK)
+        w_raw = {j0: sb.tile([P, 2, M], F32, name="w_raw%d" % j0) for j0 in (0, 2)}
         nc.vector.memset(x_plane[:].bitcast(I32), 0)
-        nc.sync.dma_start(out=w_raw[:], in_=w1.rearrange("(p j) m -> p j m", j=PACK))
+        for j0 in (0, 2):
+            nc.sync.dma_start(out=w_raw[j0][:], in_=w_rows[:, j0 : j0 + 2, :])
         nc.sync.dma_start(out=x_codes[:], in_=x_words[0])
         for q in range(4):
             (nc.scalar if q < 2 else nc.sync).dma_start(
                 out=x_plane[32 * q : 32 * q + 4, :].bitcast(I32), in_=x_scales[0, 4 * q : 4 * q + 4, :].bitcast(I32)
             )
-        nc.sync.dma_start(out=to_right[:], in_=frac)
+        nc.gpsimd.dma_start(out=to_right[:], in_=frac)
         nc.sync.dma_start(right_t[:], right)
         nc.sync.dma_start(left_t[:], left)
 
-        nc.scalar.activation(out=to_left[:], in_=to_right[:], func=COPY, scale=-1.0, bias=1.0)
+        w_cols = w_bf[:].rearrange("p (m t) -> p m t", t=PACK)
 
-        w_bf = sb.tile([P, M * PACK], BF16, name="w_bf", align_bytes=64)
-        w_codes = sb.tile([P, M], U32, name="w_codes", align_bytes=64)
-        w_plane = sb.tile([P, M], U8, name="w_plane", align_bytes=64)
-        m0 = 0
-        for n in W_CUTS:
+        def interleave(j0, m0, m1):
             nc.vector.tensor_copy(
-                out=w_bf[:, PACK * m0 : PACK * (m0 + n)].rearrange("p (c i t) -> p c t i", i=4, t=PACK),
-                in_=w_raw[:, :, m0 : m0 + n].rearrange("p t (c i) -> p c t i", i=4),
+                out=w_cols[:, m0:m1, j0 : j0 + 2].rearrange("p (c i) t -> p c t i", i=4),
+                in_=w_raw[j0][:, :, m0:m1].rearrange("p t (c i) -> p c t i", i=4),
             )
-            m0 = m0 + n
-        m0 = 0
-        for n in W_CUTS:
+
+        interleave(0, 0, M)
+        for m0 in (0, HALF):
+            interleave(2, m0, m0 + HALF)
+        for m0 in (0, HALF):
             nc.vector.quantize_mx(
-                out=w_codes[:, m0 : m0 + n].bitcast(FP8X4),
-                scales=w_plane[:, m0 : m0 + n],
-                in_=w_bf[:, PACK * m0 : PACK * (m0 + n)],
+                out=w_codes[:, m0 : m0 + HALF].bitcast(FP8X4),
+                scales=w_plane[:, m0 : m0 + HALF],
+                in_=w_bf[:, PACK * m0 : PACK * (m0 + HALF)],
             )
-            m0 = m0 + n
+        nc.scalar.activation(out=to_left[:], in_=to_right[:], func=COPY, scale=-1.0, bias=1.0)
 
         n0 = 0
         for i, n in enumerate(PASSES):
@@ -85,12 +89,11 @@ def tile_picked_wlerp_none_l_kernel(tc, x_words, x_scales, w1, frac, left, right
                 start=True,
                 stop=True,
             )
-            nc.vector.tensor_copy(out=y[:, n0 : n0 + n], in_=bank[:])
+            if i in S_BANKS:
+                nc.scalar.copy(out=y[:, n0 : n0 + n], in_=bank[:])
+            else:
+                nc.vector.tensor_copy(out=y[:, n0 : n0 + n], in_=bank[:])
             n0 = n0 + n
-
-        from_right = sb.tile([P, T], F32, name="from_right")
-        from_left = sb.tile([P, T], F32, name="from_left")
-        result = sb.tile([P, T], F32, name="result")
 
         def gather(dst, offsets, weight, v0, v1):
             nc.vector.tensor_tensor(dst[:, v0:v1], y[:].indirect(offsets[:, v0 // 16 : v1 // 16]), weight[:, v0:v1], MULT)

@@ -54,7 +54,7 @@ def tile_picked_wlerp_none_l_kernel(tc, x_words, x_scales, w1, frac, left, right
             (nc.scalar if q < 2 else nc.sync).dma_start(
                 out=x_plane[32 * q : 32 * q + 4, :].bitcast(I32), in_=x_scales[0, 4 * q : 4 * q + 4, :].bitcast(I32)
             )
-        nc.gpsimd.dma_start(out=to_right[:], in_=frac)
+        nc.sync.dma_start(out=to_right[:], in_=frac)
         nc.sync.dma_start(right_t[:], right)
         nc.sync.dma_start(left_t[:], left)
 

@@ -51,7 +51,7 @@ def tile_picked_wlerp_none_l_kernel(tc, x_words, x_scales, w1, frac, left, right
             nc.sync.dma_start(out=w_raw[j0][:], in_=w_rows[:, j0 : j0 + 2, :])
         nc.sync.dma_start(out=x_codes[:], in_=x_words[0])
         for q in range(4):
-            (nc.scalar if q < 2 else nc.sync).dma_start(
+            nc.sync.dma_start(
                 out=x_plane[32 * q : 32 * q + 4, :].bitcast(I32), in_=x_scales[0, 4 * q : 4 * q + 4, :].bitcast(I32)
             )
         nc.sync.dma_start(out=to_right[:], in_=frac)

@@ -22,6 +22,9 @@ PACK = 4
 HALF = 64
 PASSES = (128, 128, 128, 128)
 S_BANKS = ()
+EARLY = 192
+FIRST = 384
+LAST = 448
 
 
 def tile_picked_wlerp_none_l_kernel(tc, x_words, x_scales, w1, frac, left, right, out):
@@ -34,8 +37,10 @@ def tile_picked_wlerp_none_l_kernel(tc, x_words, x_scales, w1, frac, left, right
         right_t = sb.tile([P, T // 16], U16, name="right_t")
         x_codes = sb.tile([P, 2 * T], U8, name="x_codes", align_bytes=64)
         x_plane = sb.tile([P, T], U8, name="x_plane", align_bytes=64)
-        to_right = sb.tile([P, T], F32, name="to_right")
-        to_left = sb.tile([P, T], F32, name="to_left")
+        to_right = sb.tile([P, FIRST], F32, name="to_right")
+        to_right_late = sb.tile([P, T - FIRST], F32, name="to_right_late")
+        to_left = sb.tile([P, FIRST], F32, name="to_left")
+        to_left_late = sb.tile([P, T - FIRST], F32, name="to_left_late")
         y = sb.tile([P, T], F32, name="y")
         w_bf = sb.tile([P, M * PACK], BF16, name="w_bf", align_bytes=64)
         w_codes = sb.tile([P, M], U32, name="w_codes", align_bytes=64)
@@ -54,9 +59,11 @@ def tile_picked_wlerp_none_l_kernel(tc, x_words, x_scales, w1, frac, left, right
             nc.sync.dma_start(
                 out=x_plane[32 * q : 32 * q + 4, :].bitcast(I32), in_=x_scales[0, 4 * q : 4 * q + 4, :].bitcast(I32)
             )
-        nc.sync.dma_start(out=to_right[:], in_=frac)
+        nc.sync.dma_start(out=to_right[:], in_=frac[:, 0:FIRST])
         nc.sync.dma_start(right_t[:], right)
         nc.sync.dma_start(left_t[:], left)
+        nc.sync.dma_start(out=to_right_late[:, 0 : LAST - FIRST], in_=frac[:, FIRST:LAST])
+        nc.sync.dma_start(out=to_right_late[:, LAST - FIRST :], in_=frac[:, LAST:T])
 
         w_cols = w_bf[:].rearrange("p (m t) -> p m t", t=PACK)
 
@@ -96,16 +103,19 @@ def tile_picked_wlerp_none_l_kernel(tc, x_words, x_scales, w1, frac, left, right
             n0 = n0 + n
 
         def gather(dst, offsets, weight, v0, v1):
-            nc.vector.tensor_tensor(dst[:, v0:v1], y[:].indirect(offsets[:, v0 // 16 : v1 // 16]), weight[:, v0:v1], MULT)
+            nc.vector.tensor_tensor(dst[:, v0:v1], y[:].indirect(offsets[:, v0 // 16 : v1 // 16]), weight, MULT)
 
-        def finish(v0, v1):
+        def finish(*cuts):
+            v0, v1 = cuts[0], cuts[-1]
             nc.vector.tensor_tensor(result[:, v0:v1], from_left[:, v0:v1], from_right[:, v0:v1], ADD)
-            nc.sync.dma_start(out=out[:, v0:v1], in_=result[:, v0:v1])
+            for u0, u1 in zip(cuts, cuts[1:]):
+                nc.sync.dma_start(out=out[:, u0:u1], in_=result[:, u0:u1])
 
-        gather(from_right, right_t, to_right, 0, 384)
-        gather(from_left, left_t, to_left, 0, 384)
-        gather(from_right, right_t, to_right, 384, 512)
-        finish(0, 192)
-        gather(from_left, left_t, to_left, 384, 512)
-        finish(192, 384)
-        finish(384, 512)
+        gather(from_right, right_t, to_right[:], 0, FIRST)
+        gather(from_left, left_t, to_left[:], 0, FIRST)
+        nc.scalar.activation(out=to_left_late[:], in_=to_right_late[:], func=COPY, scale=-1.0, bias=1.0)
+        gather(from_right, right_t, to_right_late[:], FIRST, T)
+        finish(0, EARLY)
+        gather(from_left, left_t, to_left_late[:], FIRST, T)
+        finish(EARLY, FIRST)
+        finish(FIRST, T)

@@ -19,12 +19,12 @@ COPY = mybir.ActivationFunctionType.Copy
 
 P = 128
 PACK = 4
-HALF = 64
-PASSES = (128, 128, 128, 128)
-S_BANKS = ()
-EARLY = 192
+GROUP = 16
+HALF = M // 2
+PASS = 128
 FIRST = 384
-LAST = 448
+SUMS = (0, 192, 384, T)
+LATE = (FIRST, (FIRST + T) // 2, T)
 
 
 def tile_picked_wlerp_none_l_kernel(tc, x_words, x_scales, w1, frac, left, right, out):
@@ -33,8 +33,8 @@ def tile_picked_wlerp_none_l_kernel(tc, x_words, x_scales, w1, frac, left, right
         sb = ctx.enter_context(tc.tile_pool(name="sb", bufs=1))
         psum = ctx.enter_context(tc.psum_pool(name="psum", bufs=1))
 
-        left_t = sb.tile([P, T // 16], U16, name="left_t")
-        right_t = sb.tile([P, T // 16], U16, name="right_t")
+        left_t = sb.tile([P, T // GROUP], U16, name="left_t")
+        right_t = sb.tile([P, T // GROUP], U16, name="right_t")
         x_codes = sb.tile([P, 2 * T], U8, name="x_codes", align_bytes=64)
         x_plane = sb.tile([P, T], U8, name="x_plane", align_bytes=64)
         to_right = sb.tile([P, FIRST], F32, name="to_right")
@@ -49,11 +49,11 @@ def tile_picked_wlerp_none_l_kernel(tc, x_words, x_scales, w1, frac, left, right
         from_left = sb.tile([P, T], F32, name="from_left")
         result = sb.tile([P, T], F32, name="result")
 
-        w_rows = w1.rearrange("(p j) m -> p j m", j=PACK)
-        w_raw = {j0: sb.tile([P, 2, M], F32, name="w_raw%d" % j0) for j0 in (0, 2)}
+        w_rows = w1.rearrange("(p t) m -> p t m", t=PACK)
+        w_raw = {t0: sb.tile([P, 2, M], F32, name="w_raw%d" % t0) for t0 in (0, 2)}
         nc.vector.memset(x_plane[:].bitcast(I32), 0)
-        for j0 in (0, 2):
-            nc.sync.dma_start(out=w_raw[j0][:], in_=w_rows[:, j0 : j0 + 2, :])
+        for t0 in (0, 2):
+            nc.sync.dma_start(out=w_raw[t0][:], in_=w_rows[:, t0 : t0 + 2, :])
         nc.sync.dma_start(out=x_codes[:], in_=x_words[0])
         for q in range(4):
             nc.sync.dma_start(
@@ -62,20 +62,20 @@ def tile_picked_wlerp_none_l_kernel(tc, x_words, x_scales, w1, frac, left, right
         nc.sync.dma_start(out=to_right[:], in_=frac[:, 0:FIRST])
         nc.sync.dma_start(right_t[:], right)
         nc.sync.dma_start(left_t[:], left)
-        nc.sync.dma_start(out=to_right_late[:, 0 : LAST - FIRST], in_=frac[:, FIRST:LAST])
-        nc.sync.dma_start(out=to_right_late[:, LAST - FIRST :], in_=frac[:, LAST:T])
+        for v0, v1 in zip(LATE, LATE[1:]):
+            nc.sync.dma_start(out=to_right_late[:, v0 - FIRST : v1 - FIRST], in_=frac[:, v0:v1])
 
         w_cols = w_bf[:].rearrange("p (m t) -> p m t", t=PACK)
 
-        def interleave(j0, m0, m1):
+        def round_pair(t0, m0, m1):
             nc.vector.tensor_copy(
-                out=w_cols[:, m0:m1, j0 : j0 + 2].rearrange("p (c i) t -> p c t i", i=4),
-                in_=w_raw[j0][:, :, m0:m1].rearrange("p t (c i) -> p c t i", i=4),
+                out=w_cols[:, m0:m1, t0 : t0 + 2].rearrange("p (c i) t -> p c t i", i=4),
+                in_=w_raw[t0][:, :, m0:m1].rearrange("p t (c i) -> p c t i", i=4),
             )
 
-        interleave(0, 0, M)
+        round_pair(0, 0, M)
         for m0 in (0, HALF):
-            interleave(2, m0, m0 + HALF)
+            round_pair(2, m0, m0 + HALF)
         for m0 in (0, HALF):
             nc.vector.quantize_mx(
                 out=w_codes[:, m0 : m0 + HALF].bitcast(FP8X4),
@@ -84,38 +84,27 @@ def tile_picked_wlerp_none_l_kernel(tc, x_words, x_scales, w1, frac, left, right
             )
         nc.scalar.activation(out=to_left[:], in_=to_right[:], func=COPY, scale=-1.0, bias=1.0)
 
-        n0 = 0
-        for i, n in enumerate(PASSES):
-            bank = psum.tile([M, n], F32, name="bank%d" % i)
+        for n0 in range(0, T, PASS):
+            bank = psum.tile([M, PASS], F32, name="bank%d" % (n0 // PASS))
             nc.tensor.matmul_mx(
                 out=bank[:],
                 lhsT=w_codes[:].bitcast(FP8X4),
                 lhsT_scale=w_plane[:],
-                rhs=x_codes[:, 2 * n0 : 2 * (n0 + n)].bitcast(FP4X4),
-                rhs_scale=x_plane[:, n0 : n0 + n],
+                rhs=x_codes[:, 2 * n0 : 2 * (n0 + PASS)].bitcast(FP4X4),
+                rhs_scale=x_plane[:, n0 : n0 + PASS],
                 start=True,
                 stop=True,
             )
-            if i in S_BANKS:
-                nc.scalar.copy(out=y[:, n0 : n0 + n], in_=bank[:])
-            else:
-                nc.vector.tensor_copy(out=y[:, n0 : n0 + n], in_=bank[:])
-            n0 = n0 + n
+            nc.vector.tensor_copy(out=y[:, n0 : n0 + PASS], in_=bank[:])
 
         def gather(dst, offsets, weight, v0, v1):
-            nc.vector.tensor_tensor(dst[:, v0:v1], y[:].indirect(offsets[:, v0 // 16 : v1 // 16]), weight, MULT)
+            nc.vector.tensor_tensor(dst[:, v0:v1], y[:].indirect(offsets[:, v0 // GROUP : v1 // GROUP]), weight[:], MULT)
 
-        def finish(*cuts):
-            v0, v1 = cuts[0], cuts[-1]
-            nc.vector.tensor_tensor(result[:, v0:v1], from_left[:, v0:v1], from_right[:, v0:v1], ADD)
-            for u0, u1 in zip(cuts, cuts[1:]):
-                nc.sync.dma_start(out=out[:, u0:u1], in_=result[:, u0:u1])
-
-        gather(from_right, right_t, to_right[:], 0, FIRST)
-        gather(from_left, left_t, to_left[:], 0, FIRST)
+        gather(from_right, right_t, to_right, 0, FIRST)
+        gather(from_left, left_t, to_left, 0, FIRST)
         nc.scalar.activation(out=to_left_late[:], in_=to_right_late[:], func=COPY, scale=-1.0, bias=1.0)
-        gather(from_right, right_t, to_right_late[:], FIRST, T)
-        finish(0, EARLY)
-        gather(from_left, left_t, to_left_late[:], FIRST, T)
-        finish(EARLY, FIRST)
-        finish(FIRST, T)
+        gather(from_right, right_t, to_right_late, FIRST, T)
+        gather(from_left, left_t, to_left_late, FIRST, T)
+        for v0, v1 in zip(SUMS, SUMS[1:]):
+            nc.vector.tensor_tensor(result[:, v0:v1], from_left[:, v0:v1], from_right[:, v0:v1], ADD)
+            nc.sync.dma_start(out=out[:, v0:v1], in_=result[:, v0:v1])

@@ -50,7 +50,7 @@ def tile_picked_wlerp_none_l_kernel(tc, x_words, x_scales, w1, frac, left, right
         result = sb.tile([P, T], F32, name="result")
 
         w_rows = w1.rearrange("(p t) m -> p t m", t=PACK)
-        w_raw = {t0: sb.tile([P, 2, M], F32, name="w_raw%d" % t0) for t0 in (0, 2)}
+        w_raw = {t0: sb.tile([P, 2, M], F32, name="w_raw%d" % t0, align_bytes=256) for t0 in (0, 2)}
         nc.vector.memset(x_plane[:].bitcast(I32), 0)
         for t0 in (0, 2):
             nc.sync.dma_start(out=w_raw[t0][:], in_=w_rows[:, t0 : t0 + 2, :])

@@ -44,10 +44,10 @@ def tile_picked_wlerp_none_l_kernel(tc, x_words, x_scales, w1, frac, left, right
         y = sb.tile([P, T], F32, name="y")
         w_bf = sb.tile([P, M * PACK], BF16, name="w_bf", align_bytes=64)
         w_codes = sb.tile([P, M], U32, name="w_codes", align_bytes=64)
-        w_plane = sb.tile([P, M], U8, name="w_plane", align_bytes=64)
         from_right = sb.tile([P, T], F32, name="from_right")
         from_left = sb.tile([P, T], F32, name="from_left")
         result = sb.tile([P, T], F32, name="result")
+        w_plane = sb.tile([P, M], U8, name="w_plane", align_bytes=64)
 
         w_rows = w1.rearrange("(p t) m -> p t m", t=PACK)
         w_raw = {t0: sb.tile([P, 2, M], F32, name="w_raw%d" % t0, align_bytes=256) for t0 in (0, 2)}

@@ -22,9 +22,6 @@ PACK = 4
 GROUP = 16
 HALF = M // 2
 PASS = 128
-FIRST = 384
-SUMS = (0, 192, 384, T)
-LATE = (FIRST, (FIRST + T) // 2, T)
 
 
 def tile_picked_wlerp_none_l_kernel(tc, x_words, x_scales, w1, frac, left, right, out):
@@ -37,13 +34,13 @@ def tile_picked_wlerp_none_l_kernel(tc, x_words, x_scales, w1, frac, left, right
         right_t = sb.tile([P, T // GROUP], U16, name="right_t")
         x_codes = sb.tile([P, 2 * T], U8, name="x_codes", align_bytes=64)
         x_plane = sb.tile([P, T], U8, name="x_plane", align_bytes=64)
-        to_right = sb.tile([P, FIRST], F32, name="to_right")
-        to_right_late = sb.tile([P, T - FIRST], F32, name="to_right_late")
-        to_left = sb.tile([P, FIRST], F32, name="to_left")
-        to_left_late = sb.tile([P, T - FIRST], F32, name="to_left_late")
+        to_right = sb.tile([P, T], F32, name="to_right")
+        to_left = sb.tile([P, T], F32, name="to_left")
         y = sb.tile([P, T], F32, name="y")
         w_bf = sb.tile([P, M * PACK], BF16, name="w_bf", align_bytes=64)
         w_codes = sb.tile([P, M], U32, name="w_codes", align_bytes=64)
+        at_right = sb.tile([P, T], F32, name="at_right")
+        at_left = sb.tile([P, T], F32, name="at_left")
         from_right = sb.tile([P, T], F32, name="from_right")
         from_left = sb.tile([P, T], F32, name="from_left")
         result = sb.tile([P, T], F32, name="result")
@@ -59,11 +56,9 @@ def tile_picked_wlerp_none_l_kernel(tc, x_words, x_scales, w1, frac, left, right
             nc.sync.dma_start(
                 out=x_plane[32 * q : 32 * q + 4, :].bitcast(I32), in_=x_scales[0, 4 * q : 4 * q + 4, :].bitcast(I32)
             )
-        nc.sync.dma_start(out=to_right[:], in_=frac[:, 0:FIRST])
+        nc.sync.dma_start(out=to_right[:], in_=frac)
         nc.sync.dma_start(right_t[:], right)
         nc.sync.dma_start(left_t[:], left)
-        for v0, v1 in zip(LATE, LATE[1:]):
-            nc.sync.dma_start(out=to_right_late[:, v0 - FIRST : v1 - FIRST], in_=frac[:, v0:v1])
 
         w_cols = w_bf[:].rearrange("p (m t) -> p m t", t=PACK)
 
@@ -97,14 +92,31 @@ def tile_picked_wlerp_none_l_kernel(tc, x_words, x_scales, w1, frac, left, right
             )
             nc.vector.tensor_copy(out=y[:, n0 : n0 + PASS], in_=bank[:])
 
-        def gather(dst, offsets, weight, v0, v1):
-            nc.vector.tensor_tensor(dst[:, v0:v1], y[:].indirect(offsets[:, v0 // GROUP : v1 // GROUP]), weight[:], MULT)
+        def columns(offsets, v0, v1):
+            return y[:].indirect(offsets[:, v0 // GROUP : v1 // GROUP])
 
-        gather(from_right, right_t, to_right, 0, FIRST)
-        gather(from_left, left_t, to_left, 0, FIRST)
-        nc.scalar.activation(out=to_left_late[:], in_=to_right_late[:], func=COPY, scale=-1.0, bias=1.0)
-        gather(from_right, right_t, to_right_late, FIRST, T)
-        gather(from_left, left_t, to_left_late, FIRST, T)
-        for v0, v1 in zip(SUMS, SUMS[1:]):
+        def fetch(dst, offsets, v0, v1):
+            nc.scalar.activation(out=dst[:, v0:v1], in_=columns(offsets, v0, v1), func=COPY)
+
+        def fetch_weighted(dst, offsets, weight, v0, v1):
+            nc.vector.tensor_tensor(dst[:, v0:v1], columns(offsets, v0, v1), weight[:, v0:v1], MULT)
+
+        def weigh(dst, src, weight, v0, v1):
+            nc.vector.tensor_tensor(dst[:, v0:v1], src[:, v0:v1], weight[:, v0:v1], MULT)
+
+        def finish(v0, v1):
             nc.vector.tensor_tensor(result[:, v0:v1], from_left[:, v0:v1], from_right[:, v0:v1], ADD)
             nc.sync.dma_start(out=out[:, v0:v1], in_=result[:, v0:v1])
+
+        fetch_weighted(from_right, right_t, to_right, 0, 384)
+        fetch(at_left, left_t, 0, 192)
+        fetch(at_left, left_t, 192, 384)
+        fetch(at_right, right_t, 384, 512)
+        fetch(at_left, left_t, 384, 512)
+        weigh(from_left, at_left, to_left, 0, 192)
+        weigh(from_left, at_left, to_left, 192, 384)
+        finish(0, 192)
+        weigh(from_right, at_right, to_right, 384, 512)
+        weigh(from_left, at_left, to_left, 384, 512)
+        finish(192, 384)
+        finish(384, 512)

@@ -57,8 +57,8 @@ def tile_picked_wlerp_none_l_kernel(tc, x_words, x_scales, w1, frac, left, right
                 out=x_plane[32 * q : 32 * q + 4, :].bitcast(I32), in_=x_scales[0, 4 * q : 4 * q + 4, :].bitcast(I32)
             )
         nc.sync.dma_start(out=to_right[:], in_=frac)
-        nc.sync.dma_start(right_t[:], right)
         nc.sync.dma_start(left_t[:], left)
+        nc.sync.dma_start(right_t[:], right)
 
         w_cols = w_bf[:].rearrange("p (m t) -> p m t", t=PACK)
 
@@ -111,12 +111,12 @@ def tile_picked_wlerp_none_l_kernel(tc, x_words, x_scales, w1, frac, left, right
         fetch_weighted(from_right, right_t, to_right, 0, 384)
         fetch(at_left, left_t, 0, 192)
         fetch(at_left, left_t, 192, 384)
-        fetch(at_right, right_t, 384, 512)
         fetch(at_left, left_t, 384, 512)
+        fetch(at_right, right_t, 384, 512)
         weigh(from_left, at_left, to_left, 0, 192)
         weigh(from_left, at_left, to_left, 192, 384)
         finish(0, 192)
-        weigh(from_right, at_right, to_right, 384, 512)
         weigh(from_left, at_left, to_left, 384, 512)
+        weigh(from_right, at_right, to_right, 384, 512)
         finish(192, 384)
         finish(384, 512)

@@ -112,11 +112,10 @@ def tile_picked_wlerp_none_l_kernel(tc, x_words, x_scales, w1, frac, left, right
         fetch(at_left, left_t, 0, 192)
         fetch(at_left, left_t, 192, 384)
         fetch(at_left, left_t, 384, 512)
-        fetch(at_right, right_t, 384, 512)
         weigh(from_left, at_left, to_left, 0, 192)
+        fetch_weighted(from_right, right_t, to_right, 384, 512)
         weigh(from_left, at_left, to_left, 192, 384)
         finish(0, 192)
         weigh(from_left, at_left, to_left, 384, 512)
-        weigh(from_right, at_right, to_right, 384, 512)
         finish(192, 384)
         finish(384, 512)

@@ -22,6 +22,7 @@ PACK = 4
 GROUP = 16
 HALF = M // 2
 PASS = 128
+SUBTRACT = mybir.AluOpType.subtract
 
 
 def tile_picked_wlerp_none_l_kernel(tc, x_words, x_scales, w1, frac, left, right, out):
@@ -56,9 +57,11 @@ def tile_picked_wlerp_none_l_kernel(tc, x_words, x_scales, w1, frac, left, right
             nc.sync.dma_start(
                 out=x_plane[32 * q : 32 * q + 4, :].bitcast(I32), in_=x_scales[0, 4 * q : 4 * q + 4, :].bitcast(I32)
             )
-        nc.sync.dma_start(out=to_right[:], in_=frac)
+        nc.sync.dma_start(out=to_right[:, 0:384], in_=frac[:, 0:384])
         nc.sync.dma_start(left_t[:], left)
         nc.sync.dma_start(right_t[:], right)
+        for v0, v1 in ((384, 448), (448, 512)):
+            nc.sync.dma_start(out=to_right[:, v0:v1], in_=frac[:, v0:v1])
 
         w_cols = w_bf[:].rearrange("p (m t) -> p m t", t=PACK)
 
@@ -77,7 +80,7 @@ def tile_picked_wlerp_none_l_kernel(tc, x_words, x_scales, w1, frac, left, right
                 scales=w_plane[:, m0 : m0 + HALF],
                 in_=w_bf[:, PACK * m0 : PACK * (m0 + HALF)],
             )
-        nc.scalar.activation(out=to_left[:], in_=to_right[:], func=COPY, scale=-1.0, bias=1.0)
+        nc.scalar.activation(out=to_left[:, 0:384], in_=to_right[:, 0:384], func=COPY, scale=-1.0, bias=1.0)
 
         for n0 in range(0, T, PASS):
             bank = psum.tile([M, PASS], F32, name="bank%d" % (n0 // PASS))
@@ -104,18 +107,23 @@ def tile_picked_wlerp_none_l_kernel(tc, x_words, x_scales, w1, frac, left, right
         def weigh(dst, src, weight, v0, v1):
             nc.vector.tensor_tensor(dst[:, v0:v1], src[:, v0:v1], weight[:, v0:v1], MULT)
 
-        def finish(v0, v1):
-            nc.vector.tensor_tensor(result[:, v0:v1], from_left[:, v0:v1], from_right[:, v0:v1], ADD)
+        def weigh_negated(v0, v1):
+            nc.vector.scalar_tensor_tensor(
+                from_left[:, v0:v1], to_right[:, v0:v1], 1.0, at_left[:, v0:v1], SUBTRACT, MULT
+            )
+
+        def finish(v0, v1, op=ADD):
+            nc.vector.tensor_tensor(result[:, v0:v1], from_right[:, v0:v1], from_left[:, v0:v1], op)
             nc.sync.dma_start(out=out[:, v0:v1], in_=result[:, v0:v1])
 
         fetch_weighted(from_right, right_t, to_right, 0, 384)
+        fetch_weighted(from_right, right_t, to_right, 384, 512)
         fetch(at_left, left_t, 0, 192)
         fetch(at_left, left_t, 192, 384)
         fetch(at_left, left_t, 384, 512)
         weigh(from_left, at_left, to_left, 0, 192)
-        fetch_weighted(from_right, right_t, to_right, 384, 512)
         weigh(from_left, at_left, to_left, 192, 384)
+        weigh_negated(384, 512)
         finish(0, 192)
-        weigh(from_left, at_left, to_left, 384, 512)
         finish(192, 384)
-        finish(384, 512)
+        finish(384, 512, SUBTRACT)

@@ -37,7 +37,7 @@ def tile_picked_wlerp_none_l_kernel(tc, x_words, x_scales, w1, frac, left, right
         x_plane = sb.tile([P, T], U8, name="x_plane", align_bytes=64)
         to_right = sb.tile([P, T], F32, name="to_right")
         to_left = sb.tile([P, T], F32, name="to_left")
-        y = sb.tile([P, T], F32, name="y")
+        y = sb.tile([P, T + GROUP], F32, name="y")
         w_bf = sb.tile([P, M * PACK], BF16, name="w_bf", align_bytes=64)
         w_codes = sb.tile([P, M], U32, name="w_codes", align_bytes=64)
         at_right = sb.tile([P, T], F32, name="at_right")
@@ -52,15 +52,16 @@ def tile_picked_wlerp_none_l_kernel(tc, x_words, x_scales, w1, frac, left, right
         nc.vector.memset(x_plane[:].bitcast(I32), 0)
         for t0 in (0, 2):
             nc.sync.dma_start(out=w_raw[t0][:], in_=w_rows[:, t0 : t0 + 2, :])
-        nc.sync.dma_start(out=x_codes[:], in_=x_words[0])
         for q in range(4):
+            if q == 2:
+                nc.sync.dma_start(out=x_codes[:], in_=x_words[0])
             nc.sync.dma_start(
                 out=x_plane[32 * q : 32 * q + 4, :].bitcast(I32), in_=x_scales[0, 4 * q : 4 * q + 4, :].bitcast(I32)
             )
-        nc.sync.dma_start(out=to_right[:, 0:384], in_=frac[:, 0:384])
+        nc.sync.dma_start(out=to_right[:, 0:448], in_=frac[:, 0:448])
         nc.sync.dma_start(left_t[:], left)
         nc.sync.dma_start(right_t[:], right)
-        for v0, v1 in ((384, 448), (448, 512)):
+        for v0, v1 in ((448, 480), (480, 512)):
             nc.sync.dma_start(out=to_right[:, v0:v1], in_=frac[:, v0:v1])
 
         w_cols = w_bf[:].rearrange("p (m t) -> p m t", t=PACK)
@@ -80,7 +81,7 @@ def tile_picked_wlerp_none_l_kernel(tc, x_words, x_scales, w1, frac, left, right
                 scales=w_plane[:, m0 : m0 + HALF],
                 in_=w_bf[:, PACK * m0 : PACK * (m0 + HALF)],
             )
-        nc.scalar.activation(out=to_left[:, 0:384], in_=to_right[:, 0:384], func=COPY, scale=-1.0, bias=1.0)
+        nc.scalar.activation(out=to_left[:, 0:448], in_=to_right[:, 0:448], func=COPY, scale=1.0, bias=-1.0)
 
         for n0 in range(0, T, PASS):
             bank = psum.tile([M, PASS], F32, name="bank%d" % (n0 // PASS))
@@ -116,14 +117,13 @@ def tile_picked_wlerp_none_l_kernel(tc, x_words, x_scales, w1, frac, left, right
             nc.vector.tensor_tensor(result[:, v0:v1], from_right[:, v0:v1], from_left[:, v0:v1], op)
             nc.sync.dma_start(out=out[:, v0:v1], in_=result[:, v0:v1])
 
-        fetch_weighted(from_right, right_t, to_right, 0, 384)
-        fetch_weighted(from_right, right_t, to_right, 384, 512)
-        fetch(at_left, left_t, 0, 192)
-        fetch(at_left, left_t, 192, 384)
-        fetch(at_left, left_t, 384, 512)
-        weigh(from_left, at_left, to_left, 0, 192)
-        weigh(from_left, at_left, to_left, 192, 384)
-        weigh_negated(384, 512)
-        finish(0, 192)
-        finish(192, 384)
+        fetch_weighted(from_right, right_t, to_right, 0, 512)
+        fetch(at_left, left_t, 0, 288)
+        fetch(at_left, left_t, 288, 448)
+        fetch(at_left, left_t, 448, 512)
+        weigh(from_left, at_left, to_left, 0, 288)
+        weigh(from_left, at_left, to_left, 288, 448)
+        weigh_negated(448, 512)
+        finish(0, 192, SUBTRACT)
+        finish(192, 384, SUBTRACT)
         finish(384, 512, SUBTRACT)

@@ -14,7 +14,7 @@ U8 = mybir.dt.uint8
 FP8X4 = mybir.dt.float8_e4m3fn_x4
 FP4X4 = mybir.dt.float4_e2m1fn_x4
 MULT = mybir.AluOpType.mult
-ADD = mybir.AluOpType.add
+SUBTRACT = mybir.AluOpType.subtract
 COPY = mybir.ActivationFunctionType.Copy
 
 P = 128
@@ -22,7 +22,11 @@ PACK = 4
 GROUP = 16
 HALF = M // 2
 PASS = 128
-SUBTRACT = mybir.AluOpType.subtract
+SPARE = GROUP
+PIECES = (0, 256, 448, T)
+SUMS = (0, 192, 384, T)
+EARLY = PIECES[-2]
+LATE = (EARLY, (EARLY + T) // 2, T)
 
 
 def tile_picked_wlerp_none_l_kernel(tc, x_words, x_scales, w1, frac, left, right, out):
@@ -36,11 +40,10 @@ def tile_picked_wlerp_none_l_kernel(tc, x_words, x_scales, w1, frac, left, right
         x_codes = sb.tile([P, 2 * T], U8, name="x_codes", align_bytes=64)
         x_plane = sb.tile([P, T], U8, name="x_plane", align_bytes=64)
         to_right = sb.tile([P, T], F32, name="to_right")
-        to_left = sb.tile([P, T], F32, name="to_left")
-        y = sb.tile([P, T + GROUP], F32, name="y")
+        to_left = sb.tile([P, EARLY], F32, name="to_left")
+        y = sb.tile([P, T + SPARE], F32, name="y")
         w_bf = sb.tile([P, M * PACK], BF16, name="w_bf", align_bytes=64)
         w_codes = sb.tile([P, M], U32, name="w_codes", align_bytes=64)
-        at_right = sb.tile([P, T], F32, name="at_right")
         at_left = sb.tile([P, T], F32, name="at_left")
         from_right = sb.tile([P, T], F32, name="from_right")
         from_left = sb.tile([P, T], F32, name="from_left")
@@ -52,16 +55,21 @@ def tile_picked_wlerp_none_l_kernel(tc, x_words, x_scales, w1, frac, left, right
         nc.vector.memset(x_plane[:].bitcast(I32), 0)
         for t0 in (0, 2):
             nc.sync.dma_start(out=w_raw[t0][:], in_=w_rows[:, t0 : t0 + 2, :])
-        for q in range(4):
-            if q == 2:
-                nc.sync.dma_start(out=x_codes[:], in_=x_words[0])
+
+        def load_scale_rows(q):
             nc.sync.dma_start(
                 out=x_plane[32 * q : 32 * q + 4, :].bitcast(I32), in_=x_scales[0, 4 * q : 4 * q + 4, :].bitcast(I32)
             )
-        nc.sync.dma_start(out=to_right[:, 0:448], in_=frac[:, 0:448])
+
+        load_scale_rows(0)
+        load_scale_rows(1)
+        nc.sync.dma_start(out=x_codes[:], in_=x_words[0])
+        load_scale_rows(2)
+        load_scale_rows(3)
+        nc.sync.dma_start(out=to_right[:, 0:EARLY], in_=frac[:, 0:EARLY])
         nc.sync.dma_start(left_t[:], left)
         nc.sync.dma_start(right_t[:], right)
-        for v0, v1 in ((448, 480), (480, 512)):
+        for v0, v1 in zip(LATE, LATE[1:]):
             nc.sync.dma_start(out=to_right[:, v0:v1], in_=frac[:, v0:v1])
 
         w_cols = w_bf[:].rearrange("p (m t) -> p m t", t=PACK)
@@ -81,7 +89,7 @@ def tile_picked_wlerp_none_l_kernel(tc, x_words, x_scales, w1, frac, left, right
                 scales=w_plane[:, m0 : m0 + HALF],
                 in_=w_bf[:, PACK * m0 : PACK * (m0 + HALF)],
             )
-        nc.scalar.activation(out=to_left[:, 0:448], in_=to_right[:, 0:448], func=COPY, scale=1.0, bias=-1.0)
+        nc.scalar.activation(out=to_left[:], in_=to_right[:, 0:EARLY], func=COPY, scale=1.0, bias=-1.0)
 
         for n0 in range(0, T, PASS):
             bank = psum.tile([M, PASS], F32, name="bank%d" % (n0 // PASS))
@@ -96,34 +104,15 @@ def tile_picked_wlerp_none_l_kernel(tc, x_words, x_scales, w1, frac, left, right
             )
             nc.vector.tensor_copy(out=y[:, n0 : n0 + PASS], in_=bank[:])
 
-        def columns(offsets, v0, v1):
-            return y[:].indirect(offsets[:, v0 // GROUP : v1 // GROUP])
-
-        def fetch(dst, offsets, v0, v1):
-            nc.scalar.activation(out=dst[:, v0:v1], in_=columns(offsets, v0, v1), func=COPY)
-
-        def fetch_weighted(dst, offsets, weight, v0, v1):
-            nc.vector.tensor_tensor(dst[:, v0:v1], columns(offsets, v0, v1), weight[:, v0:v1], MULT)
-
-        def weigh(dst, src, weight, v0, v1):
-            nc.vector.tensor_tensor(dst[:, v0:v1], src[:, v0:v1], weight[:, v0:v1], MULT)
-
-        def weigh_negated(v0, v1):
-            nc.vector.scalar_tensor_tensor(
-                from_left[:, v0:v1], to_right[:, v0:v1], 1.0, at_left[:, v0:v1], SUBTRACT, MULT
-            )
-
-        def finish(v0, v1, op=ADD):
-            nc.vector.tensor_tensor(result[:, v0:v1], from_right[:, v0:v1], from_left[:, v0:v1], op)
+        nc.vector.tensor_tensor(from_right[:], y[:].indirect(right_t[:]), to_right[:], MULT)
+        for v0, v1 in zip(PIECES, PIECES[1:]):
+            offsets = left_t[:, v0 // GROUP : v1 // GROUP]
+            nc.scalar.activation(out=at_left[:, v0:v1], in_=y[:].indirect(offsets), func=COPY)
+        for v0, v1 in zip(PIECES[:-2], PIECES[1:-1]):
+            nc.vector.tensor_tensor(from_left[:, v0:v1], at_left[:, v0:v1], to_left[:, v0:v1], MULT)
+        nc.vector.scalar_tensor_tensor(
+            from_left[:, EARLY:T], to_right[:, EARLY:T], 1.0, at_left[:, EARLY:T], SUBTRACT, MULT
+        )
+        for v0, v1 in zip(SUMS, SUMS[1:]):
+            nc.vector.tensor_tensor(result[:, v0:v1], from_right[:, v0:v1], from_left[:, v0:v1], SUBTRACT)
             nc.sync.dma_start(out=out[:, v0:v1], in_=result[:, v0:v1])
-
-        fetch_weighted(from_right, right_t, to_right, 0, 512)
-        fetch(at_left, left_t, 0, 288)
-        fetch(at_left, left_t, 288, 448)
-        fetch(at_left, left_t, 448, 512)
-        weigh(from_left, at_left, to_left, 0, 288)
-        weigh(from_left, at_left, to_left, 288, 448)
-        weigh_negated(448, 512)
-        finish(0, 192, SUBTRACT)
-        finish(192, 384, SUBTRACT)
-        finish(384, 512, SUBTRACT)

@@ -51,10 +51,10 @@ def tile_picked_wlerp_none_l_kernel(tc, x_words, x_scales, w1, frac, left, right
         w_plane = sb.tile([P, M], U8, name="w_plane", align_bytes=64)
 
         w_rows = w1.rearrange("(p t) m -> p t m", t=PACK)
-        w_raw = {t0: sb.tile([P, 2, M], F32, name="w_raw%d" % t0, align_bytes=256) for t0 in (0, 2)}
+        w_raw = {m0: sb.tile([P, PACK, HALF], F32, name="w_raw%d" % m0, align_bytes=256) for m0 in (0, HALF)}
         nc.vector.memset(x_plane[:].bitcast(I32), 0)
-        for t0 in (0, 2):
-            nc.sync.dma_start(out=w_raw[t0][:], in_=w_rows[:, t0 : t0 + 2, :])
+        for m0 in (0, HALF):
+            nc.sync.dma_start(out=w_raw[m0][:], in_=w_rows[:, :, m0 : m0 + HALF])
 
         def load_scale_rows(q):
             nc.sync.dma_start(
@@ -67,22 +67,21 @@ def tile_picked_wlerp_none_l_kernel(tc, x_words, x_scales, w1, frac, left, right
         load_scale_rows(2)
         load_scale_rows(3)
         nc.sync.dma_start(out=to_right[:, 0:EARLY], in_=frac[:, 0:EARLY])
-        nc.sync.dma_start(left_t[:], left)
         nc.sync.dma_start(right_t[:], right)
         for v0, v1 in zip(LATE, LATE[1:]):
             nc.sync.dma_start(out=to_right[:, v0:v1], in_=frac[:, v0:v1])
+        nc.sync.dma_start(left_t[:], left)
 
         w_cols = w_bf[:].rearrange("p (m t) -> p m t", t=PACK)
 
-        def round_pair(t0, m0, m1):
-            nc.vector.tensor_copy(
-                out=w_cols[:, m0:m1, t0 : t0 + 2].rearrange("p (c i) t -> p c t i", i=4),
-                in_=w_raw[t0][:, :, m0:m1].rearrange("p t (c i) -> p c t i", i=4),
+        def woven(m0):
+            return (
+                w_cols[:, m0 : m0 + HALF, :].rearrange("p (c i) t -> p c t i", i=4),
+                w_raw[m0][:].rearrange("p t (c i) -> p c t i", i=4),
             )
 
-        round_pair(0, 0, M)
-        for m0 in (0, HALF):
-            round_pair(2, m0, m0 + HALF)
+        nc.scalar.copy(*woven(0))
+        nc.vector.tensor_copy(*woven(HALF))
         for m0 in (0, HALF):
             nc.vector.quantize_mx(
                 out=w_codes[:, m0 : m0 + HALF].bitcast(FP8X4),

@@ -21,6 +21,7 @@ P = 128
 PACK = 4
 GROUP = 16
 HALF = M // 2
+SHARE = 12
 PASS = 128
 SPARE = GROUP
 PIECES = (0, 256, 448, T)
@@ -50,11 +51,11 @@ def tile_picked_wlerp_none_l_kernel(tc, x_words, x_scales, w1, frac, left, right
         result = sb.tile([P, T], F32, name="result")
         w_plane = sb.tile([P, M], U8, name="w_plane", align_bytes=64)
 
-        w_rows = w1.rearrange("(p t) m -> p t m", t=PACK)
-        w_raw = {m0: sb.tile([P, PACK, HALF], F32, name="w_raw%d" % m0, align_bytes=256) for m0 in (0, HALF)}
+        w_pairs = w1.rearrange("(p u e) m -> p u (e m)", u=2, e=2)
+        w_raw = sb.tile([P, 2, 2, 3 * HALF], F32, name="w_raw", align_bytes=256)
         nc.vector.memset(x_plane[:].bitcast(I32), 0)
-        for m0 in (0, HALF):
-            nc.sync.dma_start(out=w_raw[m0][:], in_=w_rows[:, :, m0 : m0 + HALF])
+        nc.sync.dma_start(out=w_raw[:, 0], in_=w_pairs[:, :, 0 : 3 * HALF])
+        nc.sync.dma_start(out=w_raw[:, 1, :, HALF:M], in_=w_pairs[:, :, 3 * HALF : 2 * M])
 
         def load_scale_rows(q):
             nc.sync.dma_start(
@@ -72,16 +73,12 @@ def tile_picked_wlerp_none_l_kernel(tc, x_words, x_scales, w1, frac, left, right
             nc.sync.dma_start(out=to_right[:, v0:v1], in_=frac[:, v0:v1])
         nc.sync.dma_start(left_t[:], left)
 
-        w_cols = w_bf[:].rearrange("p (m t) -> p m t", t=PACK)
-
-        def woven(m0):
-            return (
-                w_cols[:, m0 : m0 + HALF, :].rearrange("p (c i) t -> p c t i", i=4),
-                w_raw[m0][:].rearrange("p t (c i) -> p c t i", i=4),
-            )
-
-        nc.scalar.copy(*woven(0))
-        nc.vector.tensor_copy(*woven(HALF))
+        w_cols = w_bf[:].rearrange("p (h c i u e) -> p h c u e i", h=2, i=4, u=2, e=2)
+        low = w_raw[:, 0].rearrange("p u (j c i) -> p c u j i", j=3, i=4)[:, :, :, 0:3:2, :]
+        high = w_raw[:, :, :, HALF:M].rearrange("p e u (c i) -> p c u e i", i=4)
+        nc.vector.tensor_copy(out=w_cols[:, 0, 0:SHARE], in_=low[:, 0:SHARE])
+        nc.scalar.copy(out=w_cols[:, 0, SHARE:], in_=low[:, SHARE:])
+        nc.vector.tensor_copy(out=w_cols[:, 1], in_=high)
         for m0 in (0, HALF):
             nc.vector.quantize_mx(
                 out=w_codes[:, m0 : m0 + HALF].bitcast(FP8X4),

from contextlib import ExitStack

import concourse.mybir as mybir

K, T, M = 512, 512, 128
FLOPS = 2 * K * T * M

F32 = mybir.dt.float32
BF16 = mybir.dt.bfloat16
I32 = mybir.dt.int32
U32 = mybir.dt.uint32
U16 = mybir.dt.uint16
U8 = mybir.dt.uint8
FP8X4 = mybir.dt.float8_e4m3fn_x4
FP4X4 = mybir.dt.float4_e2m1fn_x4
MULT = mybir.AluOpType.mult
SUBTRACT = mybir.AluOpType.subtract
COPY = mybir.ActivationFunctionType.Copy

P = 128
PACK = 4
GROUP = 16
HALF = M // 2
SHARE = 12
PASS = 128
SPARE = GROUP
PIECES = (0, 256, 448, T)
SUMS = (0, 192, 384, T)
EARLY = PIECES[-2]
LATE = (EARLY, (EARLY + T) // 2, T)


def tile_picked_wlerp_none_l_kernel(tc, x_words, x_scales, w1, frac, left, right, out):
    nc = tc.nc
    with ExitStack() as ctx:
        sb = ctx.enter_context(tc.tile_pool(name="sb", bufs=1))
        psum = ctx.enter_context(tc.psum_pool(name="psum", bufs=1))

        left_t = sb.tile([P, T // GROUP], U16, name="left_t")
        right_t = sb.tile([P, T // GROUP], U16, name="right_t")
        x_codes = sb.tile([P, 2 * T], U8, name="x_codes", align_bytes=64)
        x_plane = sb.tile([P, T], U8, name="x_plane", align_bytes=64)
        to_right = sb.tile([P, T], F32, name="to_right")
        to_left = sb.tile([P, EARLY], F32, name="to_left")
        y = sb.tile([P, T + SPARE], F32, name="y")
        w_bf = sb.tile([P, M * PACK], BF16, name="w_bf", align_bytes=64)
        w_codes = sb.tile([P, M], U32, name="w_codes", align_bytes=64)
        at_left = sb.tile([P, T], F32, name="at_left")
        from_right = sb.tile([P, T], F32, name="from_right")
        from_left = sb.tile([P, T], F32, name="from_left")
        result = sb.tile([P, T], F32, name="result")
        w_plane = sb.tile([P, M], U8, name="w_plane", align_bytes=64)

        w_pairs = w1.rearrange("(p u e) m -> p u (e m)", u=2, e=2)
        w_raw = sb.tile([P, 2, 2, 3 * HALF], F32, name="w_raw", align_bytes=256)
        nc.vector.memset(x_plane[:].bitcast(I32), 0)
        nc.sync.dma_start(out=w_raw[:, 0], in_=w_pairs[:, :, 0 : 3 * HALF])
        nc.sync.dma_start(out=w_raw[:, 1, :, HALF:M], in_=w_pairs[:, :, 3 * HALF : 2 * M])

        def load_scale_rows(q):
            nc.sync.dma_start(
                out=x_plane[32 * q : 32 * q + 4, :].bitcast(I32), in_=x_scales[0, 4 * q : 4 * q + 4, :].bitcast(I32)
            )

        load_scale_rows(0)
        load_scale_rows(1)
        nc.sync.dma_start(out=x_codes[:], in_=x_words[0])
        load_scale_rows(2)
        load_scale_rows(3)
        nc.sync.dma_start(out=to_right[:, 0:EARLY], in_=frac[:, 0:EARLY])
        nc.sync.dma_start(right_t[:], right)
        for v0, v1 in zip(LATE, LATE[1:]):
            nc.sync.dma_start(out=to_right[:, v0:v1], in_=frac[:, v0:v1])
        nc.sync.dma_start(left_t[:], left)

        w_cols = w_bf[:].rearrange("p (h c i u e) -> p h c u e i", h=2, i=4, u=2, e=2)
        low = w_raw[:, 0].rearrange("p u (j c i) -> p c u j i", j=3, i=4)[:, :, :, 0:3:2, :]
        high = w_raw[:, :, :, HALF:M].rearrange("p e u (c i) -> p c u e i", i=4)
        nc.vector.tensor_copy(out=w_cols[:, 0, 0:SHARE], in_=low[:, 0:SHARE])
        nc.scalar.copy(out=w_cols[:, 0, SHARE:], in_=low[:, SHARE:])
        nc.vector.tensor_copy(out=w_cols[:, 1], in_=high)
        for m0 in (0, HALF):
            nc.vector.quantize_mx(
                out=w_codes[:, m0 : m0 + HALF].bitcast(FP8X4),
                scales=w_plane[:, m0 : m0 + HALF],
                in_=w_bf[:, PACK * m0 : PACK * (m0 + HALF)],
            )
        nc.scalar.activation(out=to_left[:], in_=to_right[:, 0:EARLY], func=COPY, scale=1.0, bias=-1.0)

        for n0 in range(0, T, PASS):
            bank = psum.tile([M, PASS], F32, name="bank%d" % (n0 // PASS))
            nc.tensor.matmul_mx(
                out=bank[:],
                lhsT=w_codes[:].bitcast(FP8X4),
                lhsT_scale=w_plane[:],
                rhs=x_codes[:, 2 * n0 : 2 * (n0 + PASS)].bitcast(FP4X4),
                rhs_scale=x_plane[:, n0 : n0 + PASS],
                start=True,
                stop=True,
            )
            nc.vector.tensor_copy(out=y[:, n0 : n0 + PASS], in_=bank[:])

        nc.vector.tensor_tensor(from_right[:], y[:].indirect(right_t[:]), to_right[:], MULT)
        for v0, v1 in zip(PIECES, PIECES[1:]):
            offsets = left_t[:, v0 // GROUP : v1 // GROUP]
            nc.scalar.activation(out=at_left[:, v0:v1], in_=y[:].indirect(offsets), func=COPY)
        for v0, v1 in zip(PIECES[:-2], PIECES[1:-1]):
            nc.vector.tensor_tensor(from_left[:, v0:v1], at_left[:, v0:v1], to_left[:, v0:v1], MULT)
        nc.vector.scalar_tensor_tensor(
            from_left[:, EARLY:T], to_right[:, EARLY:T], 1.0, at_left[:, EARLY:T], SUBTRACT, MULT
        )
        for v0, v1 in zip(SUMS, SUMS[1:]):
            nc.vector.tensor_tensor(result[:, v0:v1], from_right[:, v0:v1], from_left[:, v0:v1], SUBTRACT)
            nc.sync.dma_start(out=out[:, v0:v1], in_=result[:, v0:v1])
